import numpy as np
import ml_dtypes


def mxq(x, axis, fmt="e4m3"):
    dtype, down = {"e4m3": (ml_dtypes.float8_e4m3fn, 7), "e5m2": (ml_dtypes.float8_e5m2, 14)}[fmt]
    v = np.moveaxis(np.asarray(x, np.float32).astype(ml_dtypes.bfloat16).astype(np.float64), axis, -1)
    blocks = v.reshape(v.shape[:-1] + (-1, 32))
    amax = np.abs(blocks).max(-1, keepdims=True)
    byte = np.maximum(np.where(amax > 0, np.frexp(amax)[1] - 1 + 127, 0) - down, 1)
    scale = np.exp2(byte - 127.0)
    codes = (blocks / scale).astype(np.float32).astype(dtype).astype(np.float64)
    return np.moveaxis((codes * scale).reshape(v.shape), -1, axis)


WIDE = False


def mx_kscale(k):
    if not WIDE:
        return np.ones(k)
    levels = np.array([10, -10, 5, -5, 0])
    if k % 512:
        return np.exp2(np.random.permutation(np.resize(levels, k // 32))).repeat(32)
    a = np.empty((k // 512, 16))
    for p in range(k // 512):
        a[p, :8] = np.random.permutation(np.resize(levels, 8))
        for g in range(8):
            far = levels[np.abs(levels - a[p, g]) >= 10]
            a[p, g + 8] = far[np.random.randint(len(far))]
    return np.exp2(a.ravel()).repeat(32)


def f64(x):
    return np.asarray(x).astype(np.float64)


def planes(y):
    n, m = y.shape
    v = y.astype(np.float32).astype(ml_dtypes.bfloat16).astype(np.float64).reshape(n // 32, 32, m)
    top = np.abs(v).max(1)
    byte = np.clip(np.where(top > 0, np.frexp(top)[1] - 1 + 127 - 7, 1), 1, 254)
    codes = (v * np.exp2(127.0 - byte)[:, None, :]).reshape(n, m).astype(np.float32).astype(ml_dtypes.float8_e4m3fn).view(np.uint8)
    words = codes.reshape(n // 512, 128, 4, m).transpose(0, 1, 3, 2)
    return np.ascontiguousarray(words), np.ascontiguousarray(byte.astype(np.uint8).reshape(n // 512, 16, m))


def split(x):
    m, e = np.frexp(f64(x))
    hi = np.ldexp(np.trunc(16.0 * m) / 16.0, e)
    return hi, f64(x) - hi


K, M, T = 2048, 512, 512


def setup_inputs():
    n = np.random.standard_normal
    s = mx_kscale(K)[:, None]
    return {
        "w": (n((K, M)) / np.sqrt(K) / s).astype(np.float32),
        "x": (n((K, T)) * s).astype(np.float32),
        "g": (n((512, 512))).astype(np.float32),
    }


def reference(w, x, g):
    w_hi, w_lo = split(w)
    w_hi_, w_lo_ = mxq(w_hi, 0, "e4m3"), mxq(w_lo, 0, "e4m3")
    x_ = mxq(f64(x), 0, "e4m3")
    y = x_.T @ w_hi_ + x_.T @ w_lo_
    out_0 = f64(g) * y
    return (out_0,) + planes(out_0)

@@ -1,0 +1,213 @@
+from contextlib import ExitStack
+
+import concourse.mybir as mybir
+
+K, M, T = 2048, 512, 512
+FLOPS = 2 * 2 * K * M * T
+
+F32 = mybir.dt.float32
+BF16 = mybir.dt.bfloat16
+I32 = mybir.dt.int32
+U32 = mybir.dt.uint32
+U8 = mybir.dt.uint8
+FP8X4 = mybir.dt.float8_e4m3fn_x4
+ALU = mybir.AluOpType
+
+P = 128
+PACK = 4
+K_PASS = P * PACK
+PASSES = K // K_PASS
+NQ = 128
+BANKS = M // NQ
+HI_MASK_PAIR = -983056
+
+
+def tile_mix_hilo_tm_pl_mul_kernel(tc, w, x, g, out_0, out_1, out_2):
+    nc = tc.nc
+
+    with ExitStack() as ctx:
+        sb = ctx.enter_context(tc.tile_pool(name="sb", bufs=1))
+        psum = ctx.enter_context(tc.psum_pool(name="psum", bufs=1))
+        ctx.enter_context(tc.manual_schedule())
+
+        def load(src, a, c0, c1, name):
+            raw = sb.tile([P, PACK, c1 - c0], F32, name=name)
+            rows = src[a * K_PASS : (a + 1) * K_PASS, c0:c1]
+            nc.sync.dma_start(out=raw[:], in_=rows.rearrange("(p j) c -> p j c", j=PACK))
+            return raw
+
+        w0a = load(w, 0, 0, 128, "w0a")
+        w0b = load(w, 0, 128, 512, "w0b")
+        w1 = load(w, 1, 0, M, "w1")
+        x0 = load(x, 0, 0, T, "x0")
+        w2 = load(w, 2, 0, M, "w2")
+        x1 = load(x, 1, 0, T, "x1")
+        w3 = load(w, 3, 0, M, "w3")
+        x2 = load(x, 2, 0, T, "x2")
+        x3 = load(x, 3, 0, T, "x3")
+        g_sb = load(g, 0, 0, M, "g_sb")
+        x_raw = [x0, x1, x2, x3]
+
+        pieces = [(0, 0, w0a[:, :, :]), (0, 128, w0b[:, :, 0:128]), (0, 256, w0b[:, :, 128:384])]
+        for a, raw in ((1, w1), (2, w2), (3, w3)):
+            pieces.append((a, 0, raw[:, :, 0:256]))
+            pieces.append((a, 256, raw[:, :, 256:512]))
+        upper, parts, w_codes, w_scales = [], [], [], []
+        for i, (a, c0, raw) in enumerate(pieces):
+            width = raw.shape[2]
+            upper.append(sb.tile([P, width * PACK], BF16, name="upper%d" % i, align_bytes=64))
+            parts.append(sb.tile([P, 2 * width * PACK], BF16, name="parts%d" % i, align_bytes=64))
+            w_codes.append(sb.tile([P, 2 * width], U32, name="w_codes%d" % i, align_bytes=64))
+            w_scales.append(sb.tile([P, 2 * width], U8, name="w_scales%d" % i, align_bytes=64))
+        x_bf, x_codes, x_scales = {}, {}, {}
+        for a in range(PASSES):
+            for h in range(2):
+                x_bf[a, h] = sb.tile([P, 2 * P * PACK], BF16, name="x_bf%d%d" % (a, h), align_bytes=64)
+                x_codes[a, h] = sb.tile([P, 2 * P], U32, name="x_codes%d%d" % (a, h), align_bytes=64)
+                x_scales[a, h] = sb.tile([P, 2 * P], U8, name="x_scales%d%d" % (a, h), align_bytes=64)
+        acc = [psum.tile([P, PACK * NQ], F32, name="acc%d" % b) for b in range(BANKS)]
+        res = [sb.tile([P, PACK, NQ], F32, name="res%d" % b) for b in range(BANKS)]
+        res_bf = [sb.tile([P, NQ * PACK], BF16, name="res_bf%d" % b, align_bytes=64) for b in range(BANKS)]
+        out_codes = sb.tile([P, M], U32, name="out_codes", align_bytes=64)
+        out_scales = sb.tile([P, M], U8, name="out_scales", align_bytes=64)
+
+        def take_upper(i):
+            raw = pieces[i][2]
+            halves = raw.bitcast(BF16).rearrange("p j (c i e) -> p c j i e", i=4, e=2)[:, :, :, :, 1]
+            nc.scalar.copy(out=upper[i][:].rearrange("p (c i j) -> p c j i", i=4, j=PACK), in_=halves)
+
+        def mask(i):
+            n = upper[i].shape[1]
+            nc.vector.tensor_scalar(
+                out=parts[i][:, 0:n].bitcast(I32),
+                in0=upper[i][:].bitcast(I32),
+                scalar1=HI_MASK_PAIR,
+                scalar2=None,
+                op0=ALU.bitwise_and,
+            )
+
+        def subtract(i):
+            n = upper[i].shape[1]
+            raw = pieces[i][2]
+            nc.vector.tensor_tensor(
+                out=parts[i][:, n : 2 * n].rearrange("p (c i j) -> p c j i", i=2, j=PACK),
+                in0=raw.rearrange("p j (c i) -> p c j i", i=2),
+                in1=parts[i][:, 0:n].rearrange("p (c i j) -> p c j i", i=2, j=PACK),
+                op=ALU.subtract,
+            )
+
+        def quantize_w(i):
+            nc.vector.quantize_mx(out=w_codes[i][:].bitcast(FP8X4), scales=w_scales[i][:], in_=parts[i][:])
+
+        def deal_x(a, h, copy):
+            src = x_raw[a][:].rearrange("p j (m r) -> p m j r", r=PACK)[:, :, :, 2 * h : 2 * h + 2]
+            copy(out=x_bf[a, h][:].rearrange("p (r m j) -> p m j r", r=2, j=PACK), in_=src)
+
+        def quantize_x(a, h):
+            nc.vector.quantize_mx(out=x_codes[a, h][:].bitcast(FP8X4), scales=x_scales[a, h][:], in_=x_bf[a, h][:])
+
+        done = [0] * BANKS
+        total = PASSES * 2 * PACK
+
+        def multiply(i, h):
+            a, c0, raw = pieces[i]
+            width = raw.shape[2]
+            for n0 in range(0, width, NQ):
+                b = (c0 + n0) // NQ
+                for rr in range(2):
+                    r = 2 * h + rr
+                    for part in range(2):
+                        cols = slice(part * width + n0, part * width + n0 + NQ)
+                        nc.tensor.matmul_mx(
+                            out=acc[b][:, r * NQ : (r + 1) * NQ],
+                            lhsT=x_codes[a, h][:, rr * P : (rr + 1) * P].bitcast(FP8X4),
+                            lhsT_scale=x_scales[a, h][:, rr * P : (rr + 1) * P],
+                            rhs=w_codes[i][:, cols].bitcast(FP8X4),
+                            rhs_scale=w_scales[i][:, cols],
+                            start=(done[b] == 0),
+                            stop=(done[b] == total - 1),
+                        )
+                        done[b] = done[b] + 1
+
+        out_rows = out_0.rearrange("(p r) n -> p r n", r=PACK)
+
+        def scale_by_g(b):
+            cols = slice(b * NQ, (b + 1) * NQ)
+            nc.vector.tensor_tensor(
+                out=res[b][:],
+                in0=acc[b][:].rearrange("p (r n) -> p r n", r=PACK),
+                in1=g_sb[:, :, cols],
+                op=ALU.mult,
+            )
+            nc.sync.dma_start(out=out_rows[:, :, cols], in_=res[b][:])
+
+        def round_result(b):
+            nc.scalar.copy(
+                out=res_bf[b][:].rearrange("p (c i r) -> p c r i", i=4, r=PACK),
+                in_=res[b][:].rearrange("p r (c i) -> p c r i", i=4),
+            )
+
+        def quantize_result(b):
+            cols = slice(b * NQ, (b + 1) * NQ)
+            nc.vector.quantize_mx(out=out_codes[:, cols].bitcast(FP8X4), scales=out_scales[:, cols], in_=res_bf[b][:])
+
+        words = out_1[0].rearrange("p n i -> p (n i)").bitcast(I32)
+        scale_rows = out_2[0].bitcast(I32)
+
+        def w_step(i):
+            take_upper(i)
+            mask(i)
+            if i > 0:
+                quantize_w(i - 1)
+            subtract(i)
+
+        def x_step(a):
+            for h in range(2):
+                deal_x(a, h, nc.scalar.copy)
+                quantize_x(a, h)
+
+        def products(a, hs):
+            for h in hs:
+                for i, piece in enumerate(pieces):
+                    if piece[0] == a:
+                        multiply(i, h)
+
+        for i in range(5):
+            w_step(i)
+        x_step(0)
+        products(0, (0, 1))
+        w_step(5)
+        w_step(6)
+        x_step(1)
+        products(1, (0, 1))
+        w_step(7)
+        deal_x(2, 0, nc.scalar.copy)
+        quantize_x(2, 0)
+        quantize_w(7)
+        deal_x(2, 1, nc.scalar.copy)
+        quantize_x(2, 1)
+        products(2, (0, 1))
+        deal_x(3, 1, nc.vector.tensor_copy)
+        take_upper(8)
+        mask(8)
+        quantize_x(3, 1)
+        multiply(7, 1)
+        subtract(8)
+        deal_x(3, 0, nc.scalar.copy)
+        quantize_x(3, 0)
+        multiply(7, 0)
+        quantize_w(8)
+        multiply(8, 1)
+        multiply(8, 0)
+
+        for b in range(BANKS):
+            scale_by_g(b)
+            round_result(b)
+        for b in range(BANKS):
+            quantize_result(b)
+            if b == BANKS - 2:
+                nc.sync.dma_start(out=words[:, 0 : 3 * NQ], in_=out_codes[:, 0 : 3 * NQ].bitcast(I32))
+        nc.scalar.dma_start(out=words[:, 3 * NQ : M], in_=out_codes[:, 3 * NQ : M].bitcast(I32))
+        for q in range(4):
+            engine = nc.sync if q % 2 == 0 else nc.scalar
+            engine.dma_start(out=scale_rows[4 * q : 4 * q + 4, :], in_=out_scales[32 * q : 32 * q + 4, :].bitcast(I32))

@@ -36,8 +36,8 @@ def tile_mix_hilo_tm_pl_mul_kernel(tc, w, x, g, out_0, out_1, out_2):
             nc.sync.dma_start(out=raw[:], in_=rows.rearrange("(p j) c -> p j c", j=PACK))
             return raw
 
-        w0a = load(w, 0, 0, 128, "w0a")
-        w0b = load(w, 0, 128, 512, "w0b")
+        w0a = load(w, 0, 0, 256, "w0a")
+        w0b = load(w, 0, 256, 512, "w0b")
         w1 = load(w, 1, 0, M, "w1")
         x0 = load(x, 0, 0, T, "x0")
         w2 = load(w, 2, 0, M, "w2")
@@ -45,10 +45,10 @@ def tile_mix_hilo_tm_pl_mul_kernel(tc, w, x, g, out_0, out_1, out_2):
         w3 = load(w, 3, 0, M, "w3")
         x2 = load(x, 2, 0, T, "x2")
         x3 = load(x, 3, 0, T, "x3")
-        g_sb = load(g, 0, 0, M, "g_sb")
+        g_half = [load(g, 0, 0, 256, "g_a"), load(g, 0, 256, 512, "g_b")]
         x_raw = [x0, x1, x2, x3]
 
-        pieces = [(0, 0, w0a[:, :, :]), (0, 128, w0b[:, :, 0:128]), (0, 256, w0b[:, :, 128:384])]
+        pieces = [(0, 0, w0a[:, :, 0:128]), (0, 128, w0a[:, :, 128:256]), (0, 256, w0b[:, :, :])]
         for a, raw in ((1, w1), (2, w2), (3, w3)):
             pieces.append((a, 0, raw[:, :, 0:256]))
             pieces.append((a, 256, raw[:, :, 256:512]))
@@ -71,10 +71,10 @@ def tile_mix_hilo_tm_pl_mul_kernel(tc, w, x, g, out_0, out_1, out_2):
         out_codes = sb.tile([P, M], U32, name="out_codes", align_bytes=64)
         out_scales = sb.tile([P, M], U8, name="out_scales", align_bytes=64)
 
-        def take_upper(i):
+        def take_upper(i, copy):
             raw = pieces[i][2]
-            halves = raw.bitcast(BF16).rearrange("p j (c i e) -> p c j i e", i=4, e=2)[:, :, :, :, 1]
-            nc.scalar.copy(out=upper[i][:].rearrange("p (c i j) -> p c j i", i=4, j=PACK), in_=halves)
+            halves = raw.bitcast(BF16).rearrange("p j (c i e) -> p c j i e", i=2, e=2)[:, :, :, :, 1]
+            copy(out=upper[i][:].rearrange("p (c i j) -> p c j i", i=2, j=PACK), in_=halves)
 
         def mask(i):
             n = upper[i].shape[1]
@@ -109,12 +109,12 @@ def tile_mix_hilo_tm_pl_mul_kernel(tc, w, x, g, out_0, out_1, out_2):
         done = [0] * BANKS
         total = PASSES * 2 * PACK
 
-        def multiply(i, h):
+        def multiply(i, hs):
             a, c0, raw = pieces[i]
             width = raw.shape[2]
             for n0 in range(0, width, NQ):
                 b = (c0 + n0) // NQ
-                for rr in range(2):
+                for h, rr in [(h, rr) for h in hs for rr in range(2)]:
                     r = 2 * h + rr
                     for part in range(2):
                         cols = slice(part * width + n0, part * width + n0 + NQ)
@@ -136,15 +136,15 @@ def tile_mix_hilo_tm_pl_mul_kernel(tc, w, x, g, out_0, out_1, out_2):
             nc.vector.tensor_tensor(
                 out=res[b][:],
                 in0=acc[b][:].rearrange("p (r n) -> p r n", r=PACK),
-                in1=g_sb[:, :, cols],
+                in1=g_half[b // 2][:, :, (b % 2) * NQ : (b % 2 + 1) * NQ],
                 op=ALU.mult,
             )
             nc.sync.dma_start(out=out_rows[:, :, cols], in_=res[b][:])
 
-        def round_result(b):
-            nc.scalar.copy(
-                out=res_bf[b][:].rearrange("p (c i r) -> p c r i", i=4, r=PACK),
-                in_=res[b][:].rearrange("p r (c i) -> p c r i", i=4),
+        def round_result(b, copy):
+            copy(
+                out=res_bf[b][:].rearrange("p (c i r) -> p c r i", i=2, r=PACK),
+                in_=res[b][:].rearrange("p r (c i) -> p c r i", i=2),
             )
 
         def quantize_result(b):
@@ -154,26 +154,39 @@ def tile_mix_hilo_tm_pl_mul_kernel(tc, w, x, g, out_0, out_1, out_2):
         words = out_1[0].rearrange("p n i -> p (n i)").bitcast(I32)
         scale_rows = out_2[0].bitcast(I32)
 
-        def w_step(i):
-            take_upper(i)
-            mask(i)
-            if i > 0:
-                quantize_w(i - 1)
-            subtract(i)
-
-        def x_step(a):
-            for h in range(2):
-                deal_x(a, h, nc.scalar.copy)
-                quantize_x(a, h)
-
         def products(a, hs):
             for h in hs:
                 for i, piece in enumerate(pieces):
                     if piece[0] == a:
-                        multiply(i, h)
+                        multiply(i, (h,))
 
-        for i in range(5):
-            w_step(i)
+        on_scalar, on_vector = nc.scalar.copy, nc.vector.tensor_copy
+
+        take_upper(0, on_vector)
+        take_upper(1, on_scalar)
+        mask(0)
+        mask(1)
+        subtract(0)
+        subtract(1)
+        take_upper(2, on_scalar)
+        mask(2)
+        quantize_w(0)
+        quantize_w(1)
+        subtract(2)
+
+        def w_step(i):
+            take_upper(i, on_scalar)
+            mask(i)
+            quantize_w(i - 1)
+            subtract(i)
+
+        def x_step(a):
+            for h in range(2):
+                deal_x(a, h, on_scalar)
+                quantize_x(a, h)
+
+        w_step(3)
+        w_step(4)
         x_step(0)
         products(0, (0, 1))
         w_step(5)
@@ -181,32 +194,34 @@ def tile_mix_hilo_tm_pl_mul_kernel(tc, w, x, g, out_0, out_1, out_2):
         x_step(1)
         products(1, (0, 1))
         w_step(7)
-        deal_x(2, 0, nc.scalar.copy)
+        deal_x(2, 0, on_scalar)
         quantize_x(2, 0)
         quantize_w(7)
-        deal_x(2, 1, nc.scalar.copy)
+        deal_x(2, 1, on_scalar)
         quantize_x(2, 1)
         products(2, (0, 1))
-        deal_x(3, 1, nc.vector.tensor_copy)
-        take_upper(8)
+        deal_x(3, 1, on_vector)
+        take_upper(8, on_scalar)
         mask(8)
         quantize_x(3, 1)
-        multiply(7, 1)
+        multiply(7, (1,))
         subtract(8)
-        deal_x(3, 0, nc.scalar.copy)
+        deal_x(3, 0, on_scalar)
         quantize_x(3, 0)
-        multiply(7, 0)
+        multiply(7, (0,))
         quantize_w(8)
-        multiply(8, 1)
-        multiply(8, 0)
+        multiply(8, (1, 0))
 
-        for b in range(BANKS):
+        for b in range(BANKS - 1):
             scale_by_g(b)
-            round_result(b)
-        for b in range(BANKS):
-            quantize_result(b)
-            if b == BANKS - 2:
-                nc.sync.dma_start(out=words[:, 0 : 3 * NQ], in_=out_codes[:, 0 : 3 * NQ].bitcast(I32))
+            round_result(b, on_scalar)
+        scale_by_g(3)
+        quantize_result(0)
+        round_result(3, on_vector)
+        quantize_result(1)
+        quantize_result(2)
+        nc.sync.dma_start(out=words[:, 0 : 3 * NQ], in_=out_codes[:, 0 : 3 * NQ].bitcast(I32))
+        quantize_result(3)
         nc.scalar.dma_start(out=words[:, 3 * NQ : M], in_=out_codes[:, 3 * NQ : M].bitcast(I32))
         for q in range(4):
             engine = nc.sync if q % 2 == 0 else nc.scalar

from contextlib import ExitStack

import concourse.mybir as mybir

K, M, T = 2048, 512, 512
FLOPS = 2 * 2 * K * M * T

F32 = mybir.dt.float32
BF16 = mybir.dt.bfloat16
I32 = mybir.dt.int32
U32 = mybir.dt.uint32
U8 = mybir.dt.uint8
FP8X4 = mybir.dt.float8_e4m3fn_x4
ALU = mybir.AluOpType

P = 128
PACK = 4
K_PASS = P * PACK
PASSES = K // K_PASS
NQ = 128
BANKS = M // NQ
HI_MASK_PAIR = -983056


def tile_mix_hilo_tm_pl_mul_kernel(tc, w, x, g, out_0, out_1, out_2):
    nc = tc.nc

    with ExitStack() as ctx:
        sb = ctx.enter_context(tc.tile_pool(name="sb", bufs=1))
        psum = ctx.enter_context(tc.psum_pool(name="psum", bufs=1))
        ctx.enter_context(tc.manual_schedule())

        def load(src, a, c0, c1, name):
            raw = sb.tile([P, PACK, c1 - c0], F32, name=name)
            rows = src[a * K_PASS : (a + 1) * K_PASS, c0:c1]
            nc.sync.dma_start(out=raw[:], in_=rows.rearrange("(p j) c -> p j c", j=PACK))
            return raw

        w0a = load(w, 0, 0, 256, "w0a")
        w0b = load(w, 0, 256, 512, "w0b")
        w1 = load(w, 1, 0, M, "w1")
        x0 = load(x, 0, 0, T, "x0")
        w2 = load(w, 2, 0, M, "w2")
        x1 = load(x, 1, 0, T, "x1")
        w3 = load(w, 3, 0, M, "w3")
        x2 = load(x, 2, 0, T, "x2")
        x3 = load(x, 3, 0, T, "x3")
        g_half = [load(g, 0, 0, 256, "g_a"), load(g, 0, 256, 512, "g_b")]
        x_raw = [x0, x1, x2, x3]

        pieces = [(0, 0, w0a[:, :, 0:128]), (0, 128, w0a[:, :, 128:256]), (0, 256, w0b[:, :, :])]
        for a, raw in ((1, w1), (2, w2), (3, w3)):
            pieces.append((a, 0, raw[:, :, 0:256]))
            pieces.append((a, 256, raw[:, :, 256:512]))
        upper, parts, w_codes, w_scales = [], [], [], []
        for i, (a, c0, raw) in enumerate(pieces):
            width = raw.shape[2]
            upper.append(sb.tile([P, width * PACK], BF16, name="upper%d" % i, align_bytes=64))
            parts.append(sb.tile([P, 2 * width * PACK], BF16, name="parts%d" % i, align_bytes=64))
            w_codes.append(sb.tile([P, 2 * width], U32, name="w_codes%d" % i, align_bytes=64))
            w_scales.append(sb.tile([P, 2 * width], U8, name="w_scales%d" % i, align_bytes=64))
        x_bf, x_codes, x_scales = {}, {}, {}
        for a in range(PASSES):
            for h in range(2):
                x_bf[a, h] = sb.tile([P, 2 * P * PACK], BF16, name="x_bf%d%d" % (a, h), align_bytes=64)
                x_codes[a, h] = sb.tile([P, 2 * P], U32, name="x_codes%d%d" % (a, h), align_bytes=64)
                x_scales[a, h] = sb.tile([P, 2 * P], U8, name="x_scales%d%d" % (a, h), align_bytes=64)
        acc = [psum.tile([P, PACK * NQ], F32, name="acc%d" % b) for b in range(BANKS)]
        res = [sb.tile([P, PACK, NQ], F32, name="res%d" % b) for b in range(BANKS)]
        res_bf = [sb.tile([P, NQ * PACK], BF16, name="res_bf%d" % b, align_bytes=64) for b in range(BANKS)]
        out_codes = sb.tile([P, M], U32, name="out_codes", align_bytes=64)
        out_scales = sb.tile([P, M], U8, name="out_scales", align_bytes=64)

        def take_upper(i, copy):
            raw = pieces[i][2]
            halves = raw.bitcast(BF16).rearrange("p j (c i e) -> p c j i e", i=2, e=2)[:, :, :, :, 1]
            copy(out=upper[i][:].rearrange("p (c i j) -> p c j i", i=2, j=PACK), in_=halves)

        def mask(i):
            n = upper[i].shape[1]
            nc.vector.tensor_scalar(
                out=parts[i][:, 0:n].bitcast(I32),
                in0=upper[i][:].bitcast(I32),
                scalar1=HI_MASK_PAIR,
                scalar2=None,
                op0=ALU.bitwise_and,
            )

        def subtract(i):
            n = upper[i].shape[1]
            raw = pieces[i][2]
            nc.vector.tensor_tensor(
                out=parts[i][:, n : 2 * n].rearrange("p (c i j) -> p c j i", i=2, j=PACK),
                in0=raw.rearrange("p j (c i) -> p c j i", i=2),
                in1=parts[i][:, 0:n].rearrange("p (c i j) -> p c j i", i=2, j=PACK),
                op=ALU.subtract,
            )

        def quantize_w(i):
            nc.vector.quantize_mx(out=w_codes[i][:].bitcast(FP8X4), scales=w_scales[i][:], in_=parts[i][:])

        def deal_x(a, h, copy):
            src = x_raw[a][:].rearrange("p j (m r) -> p m j r", r=PACK)[:, :, :, 2 * h : 2 * h + 2]
            copy(out=x_bf[a, h][:].rearrange("p (r m j) -> p m j r", r=2, j=PACK), in_=src)

        def quantize_x(a, h):
            nc.vector.quantize_mx(out=x_codes[a, h][:].bitcast(FP8X4), scales=x_scales[a, h][:], in_=x_bf[a, h][:])

        done = [0] * BANKS
        total = PASSES * 2 * PACK

        def multiply(i, hs):
            a, c0, raw = pieces[i]
            width = raw.shape[2]
            for n0 in range(0, width, NQ):
                b = (c0 + n0) // NQ
                for h, rr in [(h, rr) for h in hs for rr in range(2)]:
                    r = 2 * h + rr
                    for part in range(2):
                        cols = slice(part * width + n0, part * width + n0 + NQ)
                        nc.tensor.matmul_mx(
                            out=acc[b][:, r * NQ : (r + 1) * NQ],
                            lhsT=x_codes[a, h][:, rr * P : (rr + 1) * P].bitcast(FP8X4),
                            lhsT_scale=x_scales[a, h][:, rr * P : (rr + 1) * P],
                            rhs=w_codes[i][:, cols].bitcast(FP8X4),
                            rhs_scale=w_scales[i][:, cols],
                            start=(done[b] == 0),
                            stop=(done[b] == total - 1),
                        )
                        done[b] = done[b] + 1

        out_rows = out_0.rearrange("(p r) n -> p r n", r=PACK)

        def scale_by_g(b):
            cols = slice(b * NQ, (b + 1) * NQ)
            nc.vector.tensor_tensor(
                out=res[b][:],
                in0=acc[b][:].rearrange("p (r n) -> p r n", r=PACK),
                in1=g_half[b // 2][:, :, (b % 2) * NQ : (b % 2 + 1) * NQ],
                op=ALU.mult,
            )
            nc.sync.dma_start(out=out_rows[:, :, cols], in_=res[b][:])

        def round_result(b, copy):
            copy(
                out=res_bf[b][:].rearrange("p (c i r) -> p c r i", i=2, r=PACK),
                in_=res[b][:].rearrange("p r (c i) -> p c r i", i=2),
            )

        def quantize_result(b):
            cols = slice(b * NQ, (b + 1) * NQ)
            nc.vector.quantize_mx(out=out_codes[:, cols].bitcast(FP8X4), scales=out_scales[:, cols], in_=res_bf[b][:])

        words = out_1[0].rearrange("p n i -> p (n i)").bitcast(I32)
        scale_rows = out_2[0].bitcast(I32)

        def products(a, hs):
            for h in hs:
                for i, piece in enumerate(pieces):
                    if piece[0] == a:
                        multiply(i, (h,))

        on_scalar, on_vector = nc.scalar.copy, nc.vector.tensor_copy

        take_upper(0, on_vector)
        take_upper(1, on_scalar)
        mask(0)
        mask(1)
        subtract(0)
        subtract(1)
        take_upper(2, on_scalar)
        mask(2)
        quantize_w(0)
        quantize_w(1)
        subtract(2)

        def w_step(i):
            take_upper(i, on_scalar)
            mask(i)
            quantize_w(i - 1)
            subtract(i)

        def x_step(a):
            for h in range(2):
                deal_x(a, h, on_scalar)
                quantize_x(a, h)

        w_step(3)
        w_step(4)
        x_step(0)
        products(0, (0, 1))
        w_step(5)
        w_step(6)
        x_step(1)
        products(1, (0, 1))
        w_step(7)
        deal_x(2, 0, on_scalar)
        quantize_x(2, 0)
        quantize_w(7)
        deal_x(2, 1, on_scalar)
        quantize_x(2, 1)
        products(2, (0, 1))
        deal_x(3, 1, on_vector)
        take_upper(8, on_scalar)
        mask(8)
        quantize_x(3, 1)
        multiply(7, (1,))
        subtract(8)
        deal_x(3, 0, on_scalar)
        quantize_x(3, 0)
        multiply(7, (0,))
        quantize_w(8)
        multiply(8, (1, 0))

        for b in range(BANKS - 1):
            scale_by_g(b)
            round_result(b, on_scalar)
        scale_by_g(3)
        quantize_result(0)
        round_result(3, on_vector)
        quantize_result(1)
        quantize_result(2)
        nc.sync.dma_start(out=words[:, 0 : 3 * NQ], in_=out_codes[:, 0 : 3 * NQ].bitcast(I32))
        quantize_result(3)
        nc.scalar.dma_start(out=words[:, 3 * NQ : M], in_=out_codes[:, 3 * NQ : M].bitcast(I32))
        for q in range(4):
            engine = nc.sync if q % 2 == 0 else nc.scalar
            engine.dma_start(out=scale_rows[4 * q : 4 * q + 4, :], in_=out_scales[32 * q : 32 * q + 4, :].bitcast(I32))
